import numpy as np, ml_dtypes
CORES = [388,396,404,412,420,428,436,444,452,460,468,476,484,492,500,508,124,252,380]
N = 19
WIDTHS = [64,256,128,256,256,256,64,256,12,256,128,256,256,128,64,128,12,128,256]
XW = 256
def setup_inputs(rng):
    return {"x": rng.standard_normal((N, 128, XW), dtype=np.float32).astype(ml_dtypes.bfloat16)}
def reference(x):
    g = np.concatenate([x[r][:, :WIDTHS[r]] for r in range(N)], axis=1)
    return {"y": np.broadcast_to(g, (N,) + g.shape)}

@@ -1,0 +1,131 @@
+from concourse.bass import DstId, RemoteDMATransfer
+import comms_topo
+
+N_RANKS = 19
+TOTAL = 3160
+
+SCRATCH = {
+    "land": ("sbuf", [128, TOTAL], "bfloat16"),
+}
+SEMAPHORES = ["loaded", "stored", "sent"] + ["p%d" % r for r in range(N_RANKS)]
+
+OFF_CHIP = 0x00FF
+ENG = 8
+
+
+def _w(host, chip, core):
+    return host * 128 + chip * 8 + core
+
+
+def _balance(items, start=(0, 0)):
+    load = [start[0], start[1]]
+    out = {}
+    for key, wt in sorted(items, key=lambda kv: (-kv[1], kv[0])):
+        b = 0 if load[0] <= load[1] else 1
+        out[key] = b
+        load[b] += wt
+    return out
+
+
+def plan(cores, widths):
+    A = list(cores)
+    port = (6, 2)
+    odd = [r for r in range(1, 16, 2)] + [18]
+    even = [r for r in range(0, 16, 2)]
+    hb = {16: 1, 17: 1}
+    hb.update(_balance([(r, widths[r]) for r in odd], (0, widths[16] + widths[17])))
+    hb.update(_balance([(r, widths[r]) for r in even]))
+    gb = _balance([(r, widths[r]) for r in range(15)], (widths[17] + widths[18], 0))
+    hc = {r: port[hb[r]] for r in hb}
+    gc = {r: port[gb[r]] for r in gb}
+
+    tree = {}
+    for r in range(16):
+        c, t, kids = r, {}, []
+        for x in range(c % 2, 16, 2):
+            h = _w(3, x, hc[r])
+            kids.append(h)
+            t[h] = ([A[x]] if x != c else []) + [A[x ^ 1]]
+        if c % 2 == 0:
+            h = _w(2, 14, hc[r])
+            kids.append(h)
+            t[h] = [A[18]]
+        else:
+            kids.append(A[18])
+        if c == 15:
+            kids.append(A[16])
+            t[A[16]] = [A[17]]
+        else:
+            h = _w(0, c, gc[r])
+            kids.append(h)
+            t[h] = [A[16], A[17]]
+        t[A[r]] = kids
+        tree[r] = t
+    t = {A[18]: [_w(3, x, hc[18]) for x in range(1, 16, 2)] + [A[17]], A[17]: [A[16]]}
+    for x in range(1, 16, 2):
+        t[_w(3, x, hc[18])] = [A[x], A[x ^ 1]]
+    tree[18] = t
+    for r, other, gate_host in ((16, 17, 3), (17, 16, 2)):
+        gate = _w(gate_host, 15, hc[r])
+        t = {A[r]: [A[other], gate]}
+        kids = []
+        for x in range(1, 16, 2):
+            h = _w(3, x, hc[r])
+            if h == gate:
+                kids += [A[x], A[x ^ 1]]
+            else:
+                kids.append(h)
+                t[h] = [A[x], A[x ^ 1]]
+        kids.append(A[18])
+        t[gate] = kids
+        tree[r] = t
+
+    tasks = {}
+    for r in tree:
+        level, depth = [A[r]], 0
+        while level:
+            nxt = []
+            for node in level:
+                if node in tree[r]:
+                    tasks.setdefault(node, []).append((depth, r, tree[r][node]))
+                    nxt += tree[r][node]
+            level, depth = nxt, depth + 1
+    for c in tasks:
+        tasks[c].sort(key=lambda t3: (t3[0], t3[1]))
+    return tasks
+
+
+def rank_program(g, core, T, topo):
+    widths = T.tables["WIDTHS"]
+    offs = [sum(widths[:r]) for r in range(len(widths))]
+    tasks = plan(T.cores, widths).get(core, [])
+    rank = T.rank_of(core)
+    if rank is None and not tasks:
+        return
+
+    def piece(r):
+        return T.land[:, offs[r]:offs[r] + widths[r]]
+
+    if rank is not None:
+        g.dma_start(piece(rank), T.x[:, 0:widths[rank]]).then_inc(T.sem.loaded, 16)
+        g.wait_ge(T.sem.loaded, 16)
+
+    for depth, r, kids in tasks:
+        if depth > 0:
+            g.wait_ge(T.sem["p%d" % r], ENG)
+        ids = []
+        for d in kids:
+            rid, pid = topo.addr(d, core)
+            ids.append(DstId(rid=rid, pnc=pid))
+        g.remote_dma_fused(
+            [RemoteDMATransfer(dst_ids=ids, dma_engine_mask=OFF_CHIP, remote_sem=T.sem["p%d" % r],
+                               srcs=[piece(r)], dsts=[piece(r) for d in kids])],
+            local_sem=T.sem.sent)
+
+    if rank is not None:
+        for r in range(len(widths)):
+            if r != rank:
+                g.wait_ge(T.sem["p%d" % r], ENG)
+        g.dma_start(T.y[:, :], T.land[:, :]).then_inc(T.sem.stored, 16)
+        g.wait_ge(T.sem.stored, 16)
+    g.wait_ge(T.sem.sent, ENG * len(tasks))

@@ -6,126 +6,184 @@ TOTAL = 3160
 
 SCRATCH = {
     "land": ("sbuf", [128, TOTAL], "bfloat16"),
+    "d256_0": ("dram", [128, 256], "bfloat16"),
+    "d256_1": ("dram", [128, 256], "bfloat16"),
+    "d128_0": ("dram", [128, 128], "bfloat16"),
+    "d128_1": ("dram", [128, 128], "bfloat16"),
+    "d64_0": ("dram", [128, 64], "bfloat16"),
+    "d64_1": ("dram", [128, 64], "bfloat16"),
+    "d12_0": ("dram", [128, 12], "bfloat16"),
 }
-SEMAPHORES = ["loaded", "stored", "sent"] + ["p%d" % r for r in range(N_RANKS)]
+SEMAPHORES = ["loaded", "own", "stored", "sent"] + ["p%d" % r for r in range(N_RANKS)]
 
-OFF_CHIP = 0x00FF
-ENG = 8
+LOW, HIGH, ALL = 0x00FF, 0xFF00, 0xFFFF
+PORT_CORES = (6, 2, 7, 3)
+DIE1_CORE = 0
+GATE_CORES = (5, 1)
+STORES = 4
 
 
 def _w(host, chip, core):
     return host * 128 + chip * 8 + core
 
 
-def _balance(items, start=(0, 0)):
-    load = [start[0], start[1]]
-    out = {}
-    for key, wt in sorted(items, key=lambda kv: (-kv[1], kv[0])):
-        b = 0 if load[0] <= load[1] else 1
-        out[key] = b
-        load[b] += wt
-    return out
+def _deal(pieces, widths):
+    load, held, core, slot = [0] * 4, [[] for b in range(4)], {}, {}
+    for r in sorted(pieces, key=lambda q: (-widths[q], q)):
+        b = load.index(min(load))
+        load[b] += widths[r]
+        core[r] = PORT_CORES[b]
+        slot[r] = "d%d_%d" % (widths[r], sum(1 for q in held[b] if widths[q] == widths[r]))
+        held[b].append(r)
+    return core, slot
+
+
+def _bits(mask):
+    return bin(mask).count("1")
 
 
 def plan(cores, widths):
     A = list(cores)
-    port = (6, 2)
-    odd = [r for r in range(1, 16, 2)] + [18]
-    even = [r for r in range(0, 16, 2)]
-    hb = {16: 1, 17: 1}
-    hb.update(_balance([(r, widths[r]) for r in odd], (0, widths[16] + widths[17])))
-    hb.update(_balance([(r, widths[r]) for r in even]))
-    gb = _balance([(r, widths[r]) for r in range(15)], (widths[17] + widths[18], 0))
-    hc = {r: port[hb[r]] for r in hb}
-    gc = {r: port[gb[r]] for r in gb}
+    ranks = set(A)
+    rank_at = {(comms_topo.host(c), comms_topo.chip(c)): c for c in A}
+    kc, slot = _deal([r for r in range(1, 16, 2)] + [16, 17, 18], widths)
+    kc2, slot2 = _deal([r for r in range(0, 16, 2)], widths)
+    kc.update(kc2)
+    slot.update(slot2)
+    port_load, gate_core = [widths[17], widths[18]], {18: GATE_CORES[1]}
+    for r in sorted(range(1, 16, 2), key=lambda q: (-widths[q], q)):
+        b = 0 if port_load[0] <= port_load[1] else 1
+        port_load[b] += widths[r]
+        gate_core[r] = GATE_CORES[b]
+
+    def deliver(t, r, host, chip):
+        x = _w(host, chip, kc[r])
+        t[x] = [rank_at[p] for p in ((host, chip), (host, chip ^ 1)) if p in rank_at and rank_at[p] != A[r]]
+        return x
 
     tree = {}
-    for r in range(16):
-        c, t, kids = r, {}, []
-        for x in range(c % 2, 16, 2):
-            h = _w(3, x, hc[r])
-            kids.append(h)
-            t[h] = ([A[x]] if x != c else []) + [A[x ^ 1]]
-        if c % 2 == 0:
-            h = _w(2, 14, hc[r])
-            kids.append(h)
-            t[h] = [A[18]]
+    for r in list(range(16)) + [18]:
+        host, c = comms_topo.host(A[r]), comms_topo.chip(A[r])
+        members = [(3, x) for x in range(c % 2, 16, 2)] + [(2, 14 + c % 2)]
+        me = members.index((host, c))
+        t, die0, die1 = {}, [], []
+        for j, (h, x) in enumerate(members):
+            off = (j - me) % len(members)
+            if off == 0:
+                if (h, x ^ 1) in rank_at:
+                    die0.append(deliver(t, r, h, x))
+            elif off <= 4:
+                die0.append(deliver(t, r, h, x))
+            else:
+                die1.append(deliver(t, r, h, x))
+        second = _w(host, c, DIE1_CORE)
+        t[second] = die1
+        cabled = 3 - host
+        if c % 2:
+            gate = _w(cabled, c, gate_core[r])
+            t[gate] = [A[16], A[17]]
         else:
-            kids.append(A[18])
-        if c == 15:
-            kids.append(A[16])
-            t[A[16]] = [A[17]]
-        else:
-            h = _w(0, c, gc[r])
-            kids.append(h)
-            t[h] = [A[16], A[17]]
+            gate = _w(cabled, c, kc[r])
+            y0, y1 = _w(0, 14, kc[r]), _w(1, 14, kc[r])
+            t[y1] = [A[17]]
+            if gate == y0:
+                t[gate] = [y1, A[16]]
+            else:
+                t[gate] = [y0, y1]
+                t[y0] = [A[16]]
+        t[A[r]] = die0 + [second, gate]
+        tree[r] = t
+    for r, other in ((16, 17), (17, 16)):
+        t, kids = {}, []
+        my_host = comms_topo.host(A[r])
+        for h, x in [(0, x) for x in range(1, 16, 2)] + [(1, 15)]:
+            up = deliver(t, r, 3 - h, x)
+            if h == my_host and x == 15:
+                kids.append(up)
+            else:
+                u = _w(h, x, kc[r])
+                kids.append(u)
+                t[u] = [up] + ([A[other]] if (h, x) == (comms_topo.host(A[other]), 15) else [])
         t[A[r]] = kids
         tree[r] = t
-    t = {A[18]: [_w(3, x, hc[18]) for x in range(1, 16, 2)] + [A[17]], A[17]: [A[16]]}
-    for x in range(1, 16, 2):
-        t[_w(3, x, hc[18])] = [A[x], A[x ^ 1]]
-    tree[18] = t
-    for r, other, gate_host in ((16, 17, 3), (17, 16, 2)):
-        gate = _w(gate_host, 15, hc[r])
-        t = {A[r]: [A[other], gate]}
-        kids = []
-        for x in range(1, 16, 2):
-            h = _w(3, x, hc[r])
-            if h == gate:
-                kids += [A[x], A[x ^ 1]]
-            else:
-                kids.append(h)
-                t[h] = [A[x], A[x ^ 1]]
-        kids.append(A[18])
-        t[gate] = kids
-        tree[r] = t
 
-    tasks = {}
+    sends, arrivals = {}, {}
     for r in tree:
         level, depth = [A[r]], 0
         while level:
             nxt = []
             for node in level:
-                if node in tree[r]:
-                    tasks.setdefault(node, []).append((depth, r, tree[r][node]))
-                    nxt += tree[r][node]
+                kids = tree[r].get(node, [])
+                if not kids:
+                    continue
+                nxt += kids
+                dram = [k for k in kids if k not in ranks]
+                off = [k for k in kids if k in ranks and k // 8 != node // 8]
+                on = [k for k in kids if k in ranks and k // 8 == node // 8]
+                lows = [grp for grp in (dram, off) if grp]
+                calls = [[(grp, LOW)] for grp in lows]
+                if on and calls:
+                    calls[0].append((on, HIGH))
+                elif on:
+                    calls = [[(on, ALL)]]
+                sends.setdefault(node, []).append((depth, r, calls))
+                for call in calls:
+                    for grp, mask in call:
+                        for k in grp:
+                            arrivals.setdefault(k, {})[r] = _bits(mask)
             level, depth = nxt, depth + 1
-    for c in tasks:
-        tasks[c].sort(key=lambda t3: (t3[0], t3[1]))
-    return tasks
+    for c in sends:
+        sends[c].sort(key=lambda t3: (t3[0], t3[1]))
+    return sends, arrivals, slot
 
 
 def rank_program(g, core, T, topo):
     widths = T.tables["WIDTHS"]
-    offs = [sum(widths[:r]) for r in range(len(widths))]
-    tasks = plan(T.cores, widths).get(core, [])
+    n = len(widths)
+    offs = [sum(widths[:r]) for r in range(n + 1)]
+    sends, arrivals, slot = plan(T.cores, widths)
+    sends, arrivals = sends.get(core, []), arrivals.get(core, {})
     rank = T.rank_of(core)
-    if rank is None and not tasks:
+    ranks = set(T.cores)
+    if rank is None and not sends:
         return
 
-    def piece(r):
-        return T.land[:, offs[r]:offs[r] + widths[r]]
-
     if rank is not None:
-        g.dma_start(piece(rank), T.x[:, 0:widths[rank]]).then_inc(T.sem.loaded, 16)
+        w = widths[rank]
+        g.sync.dma_start(T[slot[rank]][:, :], T.x[:, 0:w]).then_inc(T.sem.loaded, 16)
+        g.scalar.dma_start(T.land[:, offs[rank]:offs[rank + 1]], T.x[:, 0:w]).then_inc(T.sem.own, 16)
         g.wait_ge(T.sem.loaded, 16)
 
-    for depth, r, kids in tasks:
+    left = 0
+    for depth, r, calls in sends:
         if depth > 0:
-            g.wait_ge(T.sem["p%d" % r], ENG)
-        ids = []
-        for d in kids:
-            rid, pid = topo.addr(d, core)
-            ids.append(DstId(rid=rid, pnc=pid))
-        g.remote_dma_fused(
-            [RemoteDMATransfer(dst_ids=ids, dma_engine_mask=OFF_CHIP, remote_sem=T.sem["p%d" % r],
-                               srcs=[piece(r)], dsts=[piece(r) for d in kids])],
-            local_sem=T.sem.sent)
+            g.wait_ge(T.sem["p%d" % r], arrivals[r])
+        for call in calls:
+            transfers = []
+            for grp, mask in call:
+                ids, dsts = [], []
+                for d in grp:
+                    rid, pid = topo.addr(d, core)
+                    ids.append(DstId(rid=rid, pnc=pid))
+                    dsts.append(T.land[:, offs[r]:offs[r + 1]] if d in ranks else T[slot[r]][:, :])
+                transfers.append(RemoteDMATransfer(dst_ids=ids, dma_engine_mask=mask, remote_sem=T.sem["p%d" % r],
+                                                   srcs=[T[slot[r]][:, :]], dsts=dsts))
+                left += _bits(mask)
+            g.remote_dma_fused(transfers, local_sem=T.sem.sent)
 
     if rank is not None:
-        for r in range(len(widths)):
-            if r != rank:
-                g.wait_ge(T.sem["p%d" % r], ENG)
-        g.dma_start(T.y[:, :], T.land[:, :]).then_inc(T.sem.stored, 16)
-        g.wait_ge(T.sem.stored, 16)
-    g.wait_ge(T.sem.sent, ENG * len(tasks))
+        cuts = [0]
+        for k in range(1, STORES):
+            cuts.append(min(range(cuts[-1] + 1, n), key=lambda r: abs(offs[r] - k * offs[n] // STORES)))
+        cuts.append(n)
+        for k in range(STORES):
+            q = g.sync if k % 2 == 0 else g.scalar
+            for r in range(cuts[k], cuts[k + 1]):
+                if r == rank:
+                    q.wait_ge(T.sem.own, 16)
+                else:
+                    q.wait_ge(T.sem["p%d" % r], arrivals[r])
+            a, b = offs[cuts[k]], offs[cuts[k + 1]]
+            q.dma_start(T.y[:, a:b], T.land[:, a:b]).then_inc(T.sem.stored, 16)
+        g.wait_ge(T.sem.stored, 16 * STORES)
+    g.wait_ge(T.sem.sent, left)

@@ -117,15 +117,20 @@ def plan(cores, widths):
                 if not kids:
                     continue
                 nxt += kids
-                dram = [k for k in kids if k not in ranks]
-                off = [k for k in kids if k in ranks and k // 8 != node // 8]
-                on = [k for k in kids if k in ranks and k // 8 == node // 8]
-                lows = [grp for grp in (dram, off) if grp]
-                calls = [[(grp, LOW)] for grp in lows]
-                if on and calls:
-                    calls[0].append((on, HIGH))
-                elif on:
-                    calls = [[(on, ALL)]]
+                lows, highs = [], []
+                for to_rank in (False, True):
+                    for side, on_chip in ((lows, False), (highs, True)):
+                        grp = [k for k in kids if (k in ranks) == to_rank and (k // 8 == node // 8) == on_chip]
+                        if grp:
+                            side.append(grp)
+                calls = []
+                for i in range(max(len(lows), len(highs))):
+                    if i < len(lows) and i < len(highs):
+                        calls.append([(lows[i], LOW), (highs[i], HIGH)])
+                    elif i < len(lows):
+                        calls.append([(lows[i], LOW)])
+                    else:
+                        calls.append([(highs[i], ALL)])
                 sends.setdefault(node, []).append((depth, r, calls))
                 for call in calls:
                     for grp, mask in call:

from concourse.bass import DstId, RemoteDMATransfer
import comms_topo

N_RANKS = 19
TOTAL = 3160

SCRATCH = {
    "land": ("sbuf", [128, TOTAL], "bfloat16"),
    "d256_0": ("dram", [128, 256], "bfloat16"),
    "d256_1": ("dram", [128, 256], "bfloat16"),
    "d128_0": ("dram", [128, 128], "bfloat16"),
    "d128_1": ("dram", [128, 128], "bfloat16"),
    "d64_0": ("dram", [128, 64], "bfloat16"),
    "d64_1": ("dram", [128, 64], "bfloat16"),
    "d12_0": ("dram", [128, 12], "bfloat16"),
}
SEMAPHORES = ["loaded", "own", "stored", "sent"] + ["p%d" % r for r in range(N_RANKS)]

LOW, HIGH, ALL = 0x00FF, 0xFF00, 0xFFFF
PORT_CORES = (6, 2, 7, 3)
DIE1_CORE = 0
GATE_CORES = (5, 1)
STORES = 4


def _w(host, chip, core):
    return host * 128 + chip * 8 + core


def _deal(pieces, widths):
    load, held, core, slot = [0] * 4, [[] for b in range(4)], {}, {}
    for r in sorted(pieces, key=lambda q: (-widths[q], q)):
        b = load.index(min(load))
        load[b] += widths[r]
        core[r] = PORT_CORES[b]
        slot[r] = "d%d_%d" % (widths[r], sum(1 for q in held[b] if widths[q] == widths[r]))
        held[b].append(r)
    return core, slot


def _bits(mask):
    return bin(mask).count("1")


def plan(cores, widths):
    A = list(cores)
    ranks = set(A)
    rank_at = {(comms_topo.host(c), comms_topo.chip(c)): c for c in A}
    kc, slot = _deal([r for r in range(1, 16, 2)] + [16, 17, 18], widths)
    kc2, slot2 = _deal([r for r in range(0, 16, 2)], widths)
    kc.update(kc2)
    slot.update(slot2)
    port_load, gate_core = [widths[17], widths[18]], {18: GATE_CORES[1]}
    for r in sorted(range(1, 16, 2), key=lambda q: (-widths[q], q)):
        b = 0 if port_load[0] <= port_load[1] else 1
        port_load[b] += widths[r]
        gate_core[r] = GATE_CORES[b]

    def deliver(t, r, host, chip):
        x = _w(host, chip, kc[r])
        t[x] = [rank_at[p] for p in ((host, chip), (host, chip ^ 1)) if p in rank_at and rank_at[p] != A[r]]
        return x

    tree = {}
    for r in list(range(16)) + [18]:
        host, c = comms_topo.host(A[r]), comms_topo.chip(A[r])
        members = [(3, x) for x in range(c % 2, 16, 2)] + [(2, 14 + c % 2)]
        me = members.index((host, c))
        t, die0, die1 = {}, [], []
        for j, (h, x) in enumerate(members):
            off = (j - me) % len(members)
            if off == 0:
                if (h, x ^ 1) in rank_at:
                    die0.append(deliver(t, r, h, x))
            elif off <= 4:
                die0.append(deliver(t, r, h, x))
            else:
                die1.append(deliver(t, r, h, x))
        second = _w(host, c, DIE1_CORE)
        t[second] = die1
        cabled = 3 - host
        if c % 2:
            gate = _w(cabled, c, gate_core[r])
            t[gate] = [A[16], A[17]]
        else:
            gate = _w(cabled, c, kc[r])
            y0, y1 = _w(0, 14, kc[r]), _w(1, 14, kc[r])
            t[y1] = [A[17]]
            if gate == y0:
                t[gate] = [y1, A[16]]
            else:
                t[gate] = [y0, y1]
                t[y0] = [A[16]]
        t[A[r]] = die0 + [second, gate]
        tree[r] = t
    for r, other in ((16, 17), (17, 16)):
        t, kids = {}, []
        my_host = comms_topo.host(A[r])
        for h, x in [(0, x) for x in range(1, 16, 2)] + [(1, 15)]:
            up = deliver(t, r, 3 - h, x)
            if h == my_host and x == 15:
                kids.append(up)
            else:
                u = _w(h, x, kc[r])
                kids.append(u)
                t[u] = [up] + ([A[other]] if (h, x) == (comms_topo.host(A[other]), 15) else [])
        t[A[r]] = kids
        tree[r] = t

    sends, arrivals = {}, {}
    for r in tree:
        level, depth = [A[r]], 0
        while level:
            nxt = []
            for node in level:
                kids = tree[r].get(node, [])
                if not kids:
                    continue
                nxt += kids
                lows, highs = [], []
                for to_rank in (False, True):
                    for side, on_chip in ((lows, False), (highs, True)):
                        grp = [k for k in kids if (k in ranks) == to_rank and (k // 8 == node // 8) == on_chip]
                        if grp:
                            side.append(grp)
                calls = []
                for i in range(max(len(lows), len(highs))):
                    if i < len(lows) and i < len(highs):
                        calls.append([(lows[i], LOW), (highs[i], HIGH)])
                    elif i < len(lows):
                        calls.append([(lows[i], LOW)])
                    else:
                        calls.append([(highs[i], ALL)])
                sends.setdefault(node, []).append((depth, r, calls))
                for call in calls:
                    for grp, mask in call:
                        for k in grp:
                            arrivals.setdefault(k, {})[r] = _bits(mask)
            level, depth = nxt, depth + 1
    for c in sends:
        sends[c].sort(key=lambda t3: (t3[0], t3[1]))
    return sends, arrivals, slot


def rank_program(g, core, T, topo):
    widths = T.tables["WIDTHS"]
    n = len(widths)
    offs = [sum(widths[:r]) for r in range(n + 1)]
    sends, arrivals, slot = plan(T.cores, widths)
    sends, arrivals = sends.get(core, []), arrivals.get(core, {})
    rank = T.rank_of(core)
    ranks = set(T.cores)
    if rank is None and not sends:
        return

    if rank is not None:
        w = widths[rank]
        g.sync.dma_start(T[slot[rank]][:, :], T.x[:, 0:w]).then_inc(T.sem.loaded, 16)
        g.scalar.dma_start(T.land[:, offs[rank]:offs[rank + 1]], T.x[:, 0:w]).then_inc(T.sem.own, 16)
        g.wait_ge(T.sem.loaded, 16)

    left = 0
    for depth, r, calls in sends:
        if depth > 0:
            g.wait_ge(T.sem["p%d" % r], arrivals[r])
        for call in calls:
            transfers = []
            for grp, mask in call:
                ids, dsts = [], []
                for d in grp:
                    rid, pid = topo.addr(d, core)
                    ids.append(DstId(rid=rid, pnc=pid))
                    dsts.append(T.land[:, offs[r]:offs[r + 1]] if d in ranks else T[slot[r]][:, :])
                transfers.append(RemoteDMATransfer(dst_ids=ids, dma_engine_mask=mask, remote_sem=T.sem["p%d" % r],
                                                   srcs=[T[slot[r]][:, :]], dsts=dsts))
                left += _bits(mask)
            g.remote_dma_fused(transfers, local_sem=T.sem.sent)

    if rank is not None:
        cuts = [0]
        for k in range(1, STORES):
            cuts.append(min(range(cuts[-1] + 1, n), key=lambda r: abs(offs[r] - k * offs[n] // STORES)))
        cuts.append(n)
        for k in range(STORES):
            q = g.sync if k % 2 == 0 else g.scalar
            for r in range(cuts[k], cuts[k + 1]):
                if r == rank:
                    q.wait_ge(T.sem.own, 16)
                else:
                    q.wait_ge(T.sem["p%d" % r], arrivals[r])
            a, b = offs[cuts[k]], offs[cuts[k + 1]]
            q.dma_start(T.y[:, a:b], T.land[:, a:b]).then_inc(T.sem.stored, 16)
        g.wait_ge(T.sem.stored, 16 * STORES)
    g.wait_ge(T.sem.sent, left)
